import numpy as np
import ml_dtypes


def mxq(x, axis, fmt="e4m3"):
    dtype, down = {"e4m3": (ml_dtypes.float8_e4m3fn, 7), "e5m2": (ml_dtypes.float8_e5m2, 14)}[fmt]
    v = np.moveaxis(np.asarray(x, np.float32).astype(ml_dtypes.bfloat16).astype(np.float64), axis, -1)
    blocks = v.reshape(v.shape[:-1] + (-1, 32))
    amax = np.abs(blocks).max(-1, keepdims=True)
    byte = np.maximum(np.where(amax > 0, np.frexp(amax)[1] - 1 + 127, 0) - down, 1)
    scale = np.exp2(byte - 127.0)
    codes = (blocks / scale).astype(np.float32).astype(dtype).astype(np.float64)
    return np.moveaxis((codes * scale).reshape(v.shape), -1, axis)


WIDE = False


def mx_kscale(k, group=512):
    if not WIDE:
        return np.ones(k)
    levels = np.array([10, -10, 5, -5, 0])
    if group != 512:
        return np.exp2(np.random.permutation(np.resize(levels, k // group))).repeat(group)
    if k % 512:
        return np.exp2(np.random.permutation(np.resize(levels, k // 32))).repeat(32)
    a = np.empty((k // 512, 16))
    for p in range(k // 512):
        a[p, :8] = np.random.permutation(np.resize(levels, 8))
        for g in range(8):
            far = levels[np.abs(levels - a[p, g]) >= 10]
            a[p, g + 8] = far[np.random.randint(len(far))]
    return np.exp2(a.ravel()).repeat(32)


def f64(x):
    return np.asarray(x).astype(np.float64)


def striped(idx):
    return np.tile(np.asarray(idx).reshape(-1, 16).T, (8, 1)).astype(np.uint16)


def unstriped(offs):
    return offs[:16].T.reshape(-1).astype(np.int64)


H, KV, D, NQ, N = 4, 1, 128, 512, 512
CAP = 2.0


def setup_inputs():
    n = np.random.standard_normal
    s = mx_kscale(D, 0)[:, None]
    u = mx_kscale(N)
    t = np.random.uniform(0.5, 2.0, N) * u
    v = n((KV, N, 128))
    return {
        "qT": (n((H, D, NQ)) * s * (0.70 / np.sqrt(D))).astype(np.float32),
        "kT": (n((KV, D, N)) / s).astype(np.float32),
        "t": t.reshape(N, 1).astype(np.float32),
        "v": (v / t[:, None]).astype(np.float32),
        "og": n((H, NQ, 128)).astype(np.float32),
    }


def reference(qT, kT, t, v, og):
    a = np.repeat(mxq(f64(kT), 1, "e4m3"), H // KV, 0).transpose(0, 2, 1) @ mxq(f64(qT), 1, "e4m3")
    a = CAP * np.tanh(a / CAP)
    p = np.maximum(a, 0.0)
    w = p * f64(t)
    y = mxq(w, 1, "e4m3").transpose(0, 2, 1) @ np.repeat(mxq(f64(v), 1, "e4m3"), H // KV, 0)
    y = y / 16.0
    y = y / (1.0 + np.exp(-f64(og)))
    return y

@@ -1,0 +1,220 @@
+from contextlib import ExitStack
+
+import concourse.mybir as mybir
+
+H, D, NQ, N, E = 4, 128, 512, 512, 128
+FLOPS = 2 * H * N * NQ * D + 2 * H * N * NQ * E
+
+F32 = mybir.dt.float32
+BF16 = mybir.dt.bfloat16
+U32 = mybir.dt.uint32
+I32 = mybir.dt.int32
+U8 = mybir.dt.uint8
+FP8X4 = mybir.dt.float8_e4m3fn_x4
+ACT = mybir.ActivationFunctionType
+ALU = mybir.AluOpType
+
+P = 128
+PACK = 4
+ROWS = 32
+QB = 128
+NC = NQ // QB
+K_VEC = 44
+
+
+def tile_rows_a_relu_cap_gate_kernel(tc, qT, kT, t, v, og, out):
+    nc = tc.nc
+    units = [(0, c) for c in range(NC)] + [(h, c) for c in range(NC) for h in range(1, H)]
+    groups = [[0, 1, 2, 3], [4, 5, 6], [7, 8, 9], [10, 11, 12], [13, 14], [15]]
+    group_of = {u: (g, i) for g, us in enumerate(groups) for i, u in enumerate(us)}
+
+    with ExitStack() as ctx:
+        sb = ctx.enter_context(tc.tile_pool(name="sb", bufs=1))
+        ps = ctx.enter_context(tc.psum_pool(name="ps", bufs=1))
+        ctx.enter_context(tc.manual_schedule())
+
+        def new(name, shape, dtype):
+            return sb.tile(shape, dtype, name=name, align_bytes=64)
+
+        q_rows = qT.rearrange("h (p j) n -> (h p) j n", j=PACK)
+        k_rows = kT.rearrange("o (p j) n -> (o p) j n", j=PACK)
+        og_rows = og.rearrange("h (c q) e -> q h c e", q=QB)
+        out_rows = out.rearrange("h (c q) e -> q h c e", q=QB)
+
+        q_spans = [(0, 1), (1, 2), (2, 4)]
+        q_raw = [new("q_raw%d" % i, [P, PACK, (b - a) * QB], F32) for i, (a, b) in enumerate(q_spans)]
+        q_bf = [new("q_bf%d" % i, [P, (b - a) * QB * PACK], BF16) for i, (a, b) in enumerate(q_spans)]
+        q_codes = [new("q_codes%d" % i, [P, (b - a) * QB], U32) for i, (a, b) in enumerate(q_spans)]
+        q_scales = [new("q_scales%d" % i, [P, (b - a) * QB], U8) for i, (a, b) in enumerate(q_spans)]
+        k_raw = [new("k_raw%d" % i, [ROWS, PACK, N // 2], F32) for i in range(2)]
+        k_bf = new("k_bf", [ROWS, N * PACK], BF16)
+        k_mx = new("k_mx", [P, N + N // 4], U32)
+        k_scales = k_mx[:, N:].bitcast(U8)
+        t_raw = new("t_raw", [P, PACK], F32)
+        t_twice = new("t_twice", [P, PACK], F32)
+        v_raw = new("v_raw", [P, PACK, E], F32)
+        v_bf = new("v_bf", [P, E * PACK], BF16)
+        v_codes = new("v_codes", [P, E], U32)
+        v_scales = new("v_scales", [P, E], U8)
+        og_first = new("og_first", [P, E], F32)
+        og_head0 = new("og_head0", [P, NC - 1, E], F32)
+        og_rest = [new("og_rest%d" % c, [P, H - 1, E], F32) for c in range(NC)]
+        gate_head0 = new("gate_head0", [P, NC, E], F32)
+        gate_rest = [new("gate_rest%d" % c, [P, H - 1, E], F32) for c in range(NC)]
+        capped = [new("capped%d" % u, [P, QB * PACK], F32) for u in range(len(units))]
+        w_bf = [new("w_bf%d" % u, [P, QB * PACK], BF16) for u in range(len(units))]
+        w_codes = [new("w_codes%d" % u, [P, QB], U32) for u in range(len(units))]
+        w_scales = [new("w_scales%d" % u, [P, QB], U8) for u in range(len(units))]
+        result = [new("result%d" % g, [P, len(us), E], F32) for g, us in enumerate(groups)]
+
+        score_banks = [ps.tile([P, PACK, QB], F32, name="scores%d" % i) for i in range(H + 1)]
+        y_banks = [ps.tile([P, 4, E], F32, name="y%d" % i) for i in range(3)]
+
+        def score_bank(u):
+            h, c = units[u]
+            return score_banks[c % 2] if h == 0 else score_banks[h + 1]
+
+        def load_q(i):
+            a, b = q_spans[i]
+            nc.sync.dma_start(out=q_raw[i][:], in_=q_rows[:, :, a * QB : b * QB])
+
+        def interleave(copy, dst, src):
+            copy(out=dst.rearrange("p (c i j) -> p c j i", i=4, j=PACK), in_=src.rearrange("p j (c i) -> p c j i", i=4))
+
+        def quantize(codes, scales, values):
+            nc.vector.quantize_mx(out=codes.bitcast(FP8X4), scales=scales, in_=values)
+
+        def deal_keys(copy, half, s0, s1):
+            dst = k_bf[:].rearrange("p (r s j) -> p s r j", r=PACK, j=PACK)[:, 64 * half + s0 : 64 * half + s1]
+            src = k_raw[half][:].rearrange("p j (s r) -> p s r j", r=PACK)[:, s0:s1]
+            copy(out=dst, in_=src)
+
+        def scores(u):
+            h, c = units[u]
+            i = [n for n, (a, b) in enumerate(q_spans) if a <= c < b][0]
+            cols = slice((c - q_spans[i][0]) * QB, (c - q_spans[i][0] + 1) * QB)
+            rows = slice(ROWS * h, ROWS * (h + 1))
+            for r in range(PACK):
+                toks = slice(r * P, (r + 1) * P)
+                nc.tensor.matmul_mx(
+                    out=score_bank(u)[:, r, :],
+                    lhsT=k_mx[rows, toks].bitcast(FP8X4),
+                    lhsT_scale=k_scales[rows, toks],
+                    rhs=q_codes[i][rows, cols].bitcast(FP8X4),
+                    rhs_scale=q_scales[i][rows, cols],
+                    start=True,
+                    stop=True,
+                )
+
+        def cap(u):
+            nc.scalar.activation(
+                out=capped[u][:].rearrange("p (n r) -> p n r", r=PACK),
+                in_=score_bank(u)[:].rearrange("p r n -> p n r"),
+                func=ACT.Tanh,
+                scale=0.5,
+            )
+
+        def weigh(u):
+            nc.vector.scalar_tensor_tensor(
+                out=w_bf[u][:].rearrange("p (n r) -> p n r", r=PACK),
+                in0=capped[u][:].rearrange("p (n r) -> p n r", r=PACK),
+                scalar=0.0,
+                in1=t_twice[:].unsqueeze(1).to_broadcast([P, QB, PACK]),
+                op0=ALU.max,
+                op1=ALU.mult,
+            )
+
+        def quantize_w(u):
+            quantize(w_codes[u][:], w_scales[u][:], w_bf[u][:])
+
+        def values(u):
+            g, i = group_of[u]
+            nc.tensor.matmul_mx(
+                out=y_banks[g % 3][:, i, :],
+                lhsT=w_codes[u][:].bitcast(FP8X4),
+                lhsT_scale=w_scales[u][:],
+                rhs=v_codes[:].bitcast(FP8X4),
+                rhs_scale=v_scales[:],
+                start=True,
+                stop=True,
+            )
+
+        def finish(g):
+            us = groups[g]
+            h, c = units[us[0]]
+            if h == 0:
+                gate, dst = gate_head0[:], out_rows[:, 0, :, :]
+            else:
+                gate, dst = gate_rest[c][:, h - 1 : h - 1 + len(us), :], out_rows[:, h : h + len(us), c, :]
+            nc.vector.scalar_tensor_tensor(
+                out=result[g][:],
+                in0=y_banks[g % 3][:, 0 : len(us), :],
+                scalar=1.0 / 16.0,
+                in1=gate,
+                op0=ALU.mult,
+                op1=ALU.mult,
+            )
+            nc.sync.dma_start(out=dst, in_=result[g][:])
+
+        nc.gpsimd.memset(k_mx[0:ROWS, N:], 0)
+        nc.sync.dma_start(out=og_first[:], in_=og_rows[:, 0, 0, :])
+        load_q(0)
+        for half in range(2):
+            nc.sync.dma_start(out=k_raw[half][:], in_=k_rows[:, :, half * (N // 2) : (half + 1) * (N // 2)])
+        nc.sync.dma_start(out=t_raw[:], in_=t.rearrange("(p j) o -> p (j o)", j=PACK))
+        load_q(1)
+        nc.sync.dma_start(out=v_raw[:], in_=v.rearrange("o (p j) e -> (o p) j e", j=PACK))
+        load_q(2)
+
+        nc.scalar.activation(out=gate_head0[:, 0, :], in_=og_first[:], func=ACT.Sigmoid)
+        interleave(nc.vector.tensor_copy, q_bf[0][:], q_raw[0][:])
+        deal_keys(nc.scalar.copy, 0, K_VEC, 64)
+        deal_keys(nc.vector.tensor_copy, 0, 0, K_VEC)
+        quantize(q_codes[0][:], q_scales[0][:], q_bf[0][:])
+        deal_keys(nc.scalar.copy, 1, K_VEC, 64)
+        deal_keys(nc.vector.tensor_copy, 1, 0, K_VEC)
+        nc.vector.tensor_scalar(out=t_twice[:], in0=t_raw[:], scalar1=2.0, scalar2=None, op0=ALU.mult)
+        for r in range(PACK):
+            toks = slice(r * P, (r + 1) * P)
+            quantize(k_mx[0:ROWS, toks], k_scales[0:ROWS, toks], k_bf[:, r * P * PACK : (r + 1) * P * PACK])
+        for h in range(1, H):
+            nc.sync.dma_start(out=k_mx[ROWS * h : ROWS * (h + 1), :].bitcast(I32), in_=k_mx[0:ROWS, :].bitcast(I32))
+        nc.sync.dma_start(out=og_head0[:], in_=og_rows[:, 0, 1:, :])
+        for c in range(NC):
+            nc.sync.dma_start(out=og_rest[c][:], in_=og_rows[:, 1:, c, :])
+
+        scores(0)
+        interleave(nc.scalar.copy, v_bf[:], v_raw[:])
+        interleave(nc.vector.tensor_copy, q_bf[1][:], q_raw[1][:])
+        interleave(nc.vector.tensor_copy, q_bf[2][:], q_raw[2][:])
+        quantize(q_codes[1][:], q_scales[1][:], q_bf[1][:])
+        scores(1)
+        cap(0)
+        quantize(q_codes[2][:], q_scales[2][:], q_bf[2][:])
+        quantize(v_codes[:], v_scales[:], v_bf[:])
+        cap(1)
+        for u in range(2, 4):
+            scores(u)
+            cap(u)
+        nc.scalar.activation(out=gate_head0[:, 1:, :], in_=og_head0[:], func=ACT.Sigmoid)
+
+        ahead = 4
+        last = len(units) - 1
+        weigh(0)
+        for u in range(len(units)):
+            n = u + ahead
+            if n <= last:
+                scores(n)
+                cap(n)
+                h, c = units[n]
+                if h == H - 1:
+                    nc.scalar.activation(out=gate_rest[c][:], in_=og_rest[c][:], func=ACT.Sigmoid)
+            if u < last:
+                weigh(u + 1)
+            quantize_w(u)
+            values(u)
+            for g in range(4):
+                if groups[g][-1] == u - 1:
+                    finish(g)
+        finish(4)
+        finish(5)

@@ -19,13 +19,14 @@ PACK = 4
 ROWS = 32
 QB = 128
 NC = NQ // QB
-K_VEC = 44
 
 
 def tile_rows_a_relu_cap_gate_kernel(tc, qT, kT, t, v, og, out):
     nc = tc.nc
-    units = [(0, c) for c in range(NC)] + [(h, c) for c in range(NC) for h in range(1, H)]
-    groups = [[0, 1, 2, 3], [4, 5, 6], [7, 8, 9], [10, 11, 12], [13, 14], [15]]
+    others = lambda c: [(h, c) for h in range(1, H)]
+    units = [(0, 0), (0, 1)] + others(0) + [(0, 2)] + others(1) + [(0, 3)] + others(2) + others(3)
+    last = len(units) - 1
+    groups = [[0, 1], [2, 3, 4, 5], [6, 7, 8, 9], [10, 11, 12], [13, 14], [15]]
     group_of = {u: (g, i) for g, us in enumerate(groups) for i, u in enumerate(us)}
 
     with ExitStack() as ctx:
@@ -41,11 +42,10 @@ def tile_rows_a_relu_cap_gate_kernel(tc, qT, kT, t, v, og, out):
         og_rows = og.rearrange("h (c q) e -> q h c e", q=QB)
         out_rows = out.rearrange("h (c q) e -> q h c e", q=QB)
 
-        q_spans = [(0, 1), (1, 2), (2, 4)]
-        q_raw = [new("q_raw%d" % i, [P, PACK, (b - a) * QB], F32) for i, (a, b) in enumerate(q_spans)]
-        q_bf = [new("q_bf%d" % i, [P, (b - a) * QB * PACK], BF16) for i, (a, b) in enumerate(q_spans)]
-        q_codes = [new("q_codes%d" % i, [P, (b - a) * QB], U32) for i, (a, b) in enumerate(q_spans)]
-        q_scales = [new("q_scales%d" % i, [P, (b - a) * QB], U8) for i, (a, b) in enumerate(q_spans)]
+        q_raw = [new("q_raw%d" % c, [P, PACK, QB], F32) for c in range(NC)]
+        q_bf = [new("q_bf%d" % c, [P, QB * PACK], BF16) for c in range(NC)]
+        q_codes = [new("q_codes%d" % c, [P, QB], U32) for c in range(NC)]
+        q_scales = [new("q_scales%d" % c, [P, QB], U8) for c in range(NC)]
         k_raw = [new("k_raw%d" % i, [ROWS, PACK, N // 2], F32) for i in range(2)]
         k_bf = new("k_bf", [ROWS, N * PACK], BF16)
         k_mx = new("k_mx", [P, N + N // 4], U32)
@@ -59,8 +59,7 @@ def tile_rows_a_relu_cap_gate_kernel(tc, qT, kT, t, v, og, out):
         og_first = new("og_first", [P, E], F32)
         og_head0 = new("og_head0", [P, NC - 1, E], F32)
         og_rest = [new("og_rest%d" % c, [P, H - 1, E], F32) for c in range(NC)]
-        gate_head0 = new("gate_head0", [P, NC, E], F32)
-        gate_rest = [new("gate_rest%d" % c, [P, H - 1, E], F32) for c in range(NC)]
+        gate = new("gate", [P, len(units) * E], F32)
         capped = [new("capped%d" % u, [P, QB * PACK], F32) for u in range(len(units))]
         w_bf = [new("w_bf%d" % u, [P, QB * PACK], BF16) for u in range(len(units))]
         w_codes = [new("w_codes%d" % u, [P, QB], U32) for u in range(len(units))]
@@ -74,9 +73,8 @@ def tile_rows_a_relu_cap_gate_kernel(tc, qT, kT, t, v, og, out):
             h, c = units[u]
             return score_banks[c % 2] if h == 0 else score_banks[h + 1]
 
-        def load_q(i):
-            a, b = q_spans[i]
-            nc.sync.dma_start(out=q_raw[i][:], in_=q_rows[:, :, a * QB : b * QB])
+        def load_q(c):
+            nc.sync.dma_start(out=q_raw[c][:], in_=q_rows[:, :, c * QB : (c + 1) * QB])
 
         def interleave(copy, dst, src):
             copy(out=dst.rearrange("p (c i j) -> p c j i", i=4, j=PACK), in_=src.rearrange("p j (c i) -> p c j i", i=4))
@@ -84,27 +82,26 @@ def tile_rows_a_relu_cap_gate_kernel(tc, qT, kT, t, v, og, out):
         def quantize(codes, scales, values):
             nc.vector.quantize_mx(out=codes.bitcast(FP8X4), scales=scales, in_=values)
 
-        def deal_keys(copy, half, s0, s1):
-            dst = k_bf[:].rearrange("p (r s j) -> p s r j", r=PACK, j=PACK)[:, 64 * half + s0 : 64 * half + s1]
-            src = k_raw[half][:].rearrange("p j (s r) -> p s r j", r=PACK)[:, s0:s1]
-            copy(out=dst, in_=src)
+        def quantize_q(c):
+            quantize(q_codes[c][:], q_scales[c][:], q_bf[c][:])
 
-        def scores(u):
+        def deal_keys(half):
+            dst = k_bf[:].rearrange("p (r s j) -> p s r j", r=PACK, j=PACK)[:, 64 * half : 64 * (half + 1)]
+            nc.vector.tensor_copy(out=dst, in_=k_raw[half][:].rearrange("p j (s r) -> p s r j", r=PACK))
+
+        def scores(u, r):
             h, c = units[u]
-            i = [n for n, (a, b) in enumerate(q_spans) if a <= c < b][0]
-            cols = slice((c - q_spans[i][0]) * QB, (c - q_spans[i][0] + 1) * QB)
             rows = slice(ROWS * h, ROWS * (h + 1))
-            for r in range(PACK):
-                toks = slice(r * P, (r + 1) * P)
-                nc.tensor.matmul_mx(
-                    out=score_bank(u)[:, r, :],
-                    lhsT=k_mx[rows, toks].bitcast(FP8X4),
-                    lhsT_scale=k_scales[rows, toks],
-                    rhs=q_codes[i][rows, cols].bitcast(FP8X4),
-                    rhs_scale=q_scales[i][rows, cols],
-                    start=True,
-                    stop=True,
-                )
+            toks = slice(r * P, (r + 1) * P)
+            nc.tensor.matmul_mx(
+                out=score_bank(u)[:, r, :],
+                lhsT=k_mx[rows, toks].bitcast(FP8X4),
+                lhsT_scale=k_scales[rows, toks],
+                rhs=q_codes[c][rows, :].bitcast(FP8X4),
+                rhs_scale=q_scales[c][rows, :],
+                start=True,
+                stop=True,
+            )
 
         def cap(u):
             nc.scalar.activation(
@@ -139,82 +136,100 @@ def tile_rows_a_relu_cap_gate_kernel(tc, qT, kT, t, v, og, out):
                 stop=True,
             )
 
-        def finish(g):
+        def sigmoid_others(c):
+            u = units.index((1, c))
+            nc.scalar.activation(
+                out=gate[:, u * E : (u + H - 1) * E], in_=og_rest[c][:].rearrange("p h e -> p (h e)"), func=ACT.Sigmoid
+            )
+
+        def finish(g, queue):
             us = groups[g]
-            h, c = units[us[0]]
-            if h == 0:
-                gate, dst = gate_head0[:], out_rows[:, 0, :, :]
-            else:
-                gate, dst = gate_rest[c][:, h - 1 : h - 1 + len(us), :], out_rows[:, h : h + len(us), c, :]
             nc.vector.scalar_tensor_tensor(
-                out=result[g][:],
-                in0=y_banks[g % 3][:, 0 : len(us), :],
+                out=result[g][:].rearrange("p u e -> p (u e)"),
+                in0=y_banks[g % 3][:, 0 : len(us), :].rearrange("p u e -> p (u e)"),
                 scalar=1.0 / 16.0,
-                in1=gate,
+                in1=gate[:, us[0] * E : (us[-1] + 1) * E],
                 op0=ALU.mult,
                 op1=ALU.mult,
             )
-            nc.sync.dma_start(out=dst, in_=result[g][:])
+            rest = [i for i, u in enumerate(us) if units[u][0] > 0]
+            zero = [i for i, u in enumerate(us) if units[u][0] == 0]
+            if rest:
+                h, c = units[us[rest[0]]]
+                queue.dma_start(out=out_rows[:, h : h + len(rest), c, :], in_=result[g][:, rest[0] : rest[-1] + 1, :])
+            if zero:
+                c = units[us[zero[0]]][1]
+                queue.dma_start(out=out_rows[:, 0, c : c + len(zero), :], in_=result[g][:, zero[0] : zero[-1] + 1, :])
 
         nc.gpsimd.memset(k_mx[0:ROWS, N:], 0)
-        nc.sync.dma_start(out=og_first[:], in_=og_rows[:, 0, 0, :])
-        load_q(0)
         for half in range(2):
             nc.sync.dma_start(out=k_raw[half][:], in_=k_rows[:, :, half * (N // 2) : (half + 1) * (N // 2)])
-        nc.sync.dma_start(out=t_raw[:], in_=t.rearrange("(p j) o -> p (j o)", j=PACK))
-        load_q(1)
-        nc.sync.dma_start(out=v_raw[:], in_=v.rearrange("o (p j) e -> (o p) j e", j=PACK))
-        load_q(2)
+        nc.scalar.dma_start(out=og_first[:], in_=og_rows[:, 0, 0, :])
+        nc.scalar.dma_start(out=t_raw[:], in_=t.rearrange("(p j) o -> p (j o)", j=PACK))
+        for c in range(3):
+            load_q(c)
 
-        nc.scalar.activation(out=gate_head0[:, 0, :], in_=og_first[:], func=ACT.Sigmoid)
-        interleave(nc.vector.tensor_copy, q_bf[0][:], q_raw[0][:])
-        deal_keys(nc.scalar.copy, 0, K_VEC, 64)
-        deal_keys(nc.vector.tensor_copy, 0, 0, K_VEC)
-        quantize(q_codes[0][:], q_scales[0][:], q_bf[0][:])
-        deal_keys(nc.scalar.copy, 1, K_VEC, 64)
-        deal_keys(nc.vector.tensor_copy, 1, 0, K_VEC)
-        nc.vector.tensor_scalar(out=t_twice[:], in0=t_raw[:], scalar1=2.0, scalar2=None, op0=ALU.mult)
-        for r in range(PACK):
-            toks = slice(r * P, (r + 1) * P)
-            quantize(k_mx[0:ROWS, toks], k_scales[0:ROWS, toks], k_bf[:, r * P * PACK : (r + 1) * P * PACK])
+        nc.scalar.activation(out=gate[:, 0:E], in_=og_first[:], func=ACT.Sigmoid)
+        nc.scalar.mul(out=t_twice[:], in_=t_raw[:], mul=2.0)
+        interleave(nc.scalar.copy, q_bf[0][:], q_raw[0][:])
+        deal_keys(0)
+        deal_keys(1)
+        quantize(k_mx[0:ROWS, 0:N], k_scales[0:ROWS, :], k_bf[:])
+        quantize_q(0)
         for h in range(1, H):
             nc.sync.dma_start(out=k_mx[ROWS * h : ROWS * (h + 1), :].bitcast(I32), in_=k_mx[0:ROWS, :].bitcast(I32))
+        nc.sync.dma_start(out=v_raw[:], in_=v.rearrange("o (p j) e -> (o p) j e", j=PACK))
+        load_q(3)
         nc.sync.dma_start(out=og_head0[:], in_=og_rows[:, 0, 1:, :])
         for c in range(NC):
             nc.sync.dma_start(out=og_rest[c][:], in_=og_rows[:, 1:, c, :])
 
-        scores(0)
-        interleave(nc.scalar.copy, v_bf[:], v_raw[:])
         interleave(nc.vector.tensor_copy, q_bf[1][:], q_raw[1][:])
+        quantize_q(1)
         interleave(nc.vector.tensor_copy, q_bf[2][:], q_raw[2][:])
-        quantize(q_codes[1][:], q_scales[1][:], q_bf[1][:])
-        scores(1)
-        cap(0)
-        quantize(q_codes[2][:], q_scales[2][:], q_bf[2][:])
-        quantize(v_codes[:], v_scales[:], v_bf[:])
-        cap(1)
-        for u in range(2, 4):
-            scores(u)
-            cap(u)
-        nc.scalar.activation(out=gate_head0[:, 1:, :], in_=og_head0[:], func=ACT.Sigmoid)
+        for u in range(3):
+            for r in range(PACK):
+                scores(u, r)
 
-        ahead = 4
-        last = len(units) - 1
-        weigh(0)
-        for u in range(len(units)):
-            n = u + ahead
-            if n <= last:
-                scores(n)
-                cap(n)
-                h, c = units[n]
-                if h == H - 1:
-                    nc.scalar.activation(out=gate_rest[c][:], in_=og_rest[c][:], func=ACT.Sigmoid)
-            if u < last:
-                weigh(u + 1)
-            quantize_w(u)
-            values(u)
-            for g in range(4):
-                if groups[g][-1] == u - 1:
-                    finish(g)
-        finish(4)
-        finish(5)
+        for step in range(len(units)):
+            cap(step)
+            for r in range(2):
+                if step + 3 <= last:
+                    scores(step + 3, r)
+                if 3 <= step + 2 <= last:
+                    scores(step + 2, r + 2)
+            if step == 3:
+                interleave(nc.scalar.copy, v_bf[:], v_raw[:])
+            if step == 5:
+                nc.scalar.activation(
+                    out=gate[:].rearrange("p (a u e) -> p a u e", u=4, e=E)[:, 0:3, 1, :], in_=og_head0[:], func=ACT.Sigmoid
+                )
+            if step in (7, 10, 12, 14):
+                sigmoid_others((7, 10, 12, 14).index(step))
+            weigh(step)
+            if step == 0:
+                quantize_q(2)
+            if step > 0:
+                quantize_w(step - 1)
+            if step == 3:
+                interleave(nc.vector.tensor_copy, q_bf[3][:], q_raw[3][:])
+            if step == 4:
+                quantize_q(3)
+            if step == 5:
+                quantize(v_codes[:], v_scales[:], v_bf[:])
+            if step in (6, 8, 12):
+                g = (6, 8, 12).index(step)
+                for u in groups[g]:
+                    values(u)
+                finish(g, nc.sync)
+            if step == 13:
+                for u in groups[3]:
+                    values(u)
+            if step == 14:
+                finish(3, nc.sync)
+            if step >= 14:
+                values(step - 1)
+        quantize_w(last)
+        values(last)
+        finish(4, nc.sync)
+        finish(5, nc.scalar)

@@ -16,17 +16,28 @@ ALU = mybir.AluOpType
 
 P = 128
 PACK = 4
-ROWS = 32
+ROWS = D // PACK
 QB = 128
-NC = NQ // QB
+WIDE = QB * PACK
+BANK_UNITS = 4
+Y_BANKS = 3
+
+Q_PARTS = [(0, 1), (1, 2), (2, 4)]
+VALUES_LAG = 3
+FINISH_LAG = 4
+SIGMOID_LEAD = 2
 
 
 def tile_rows_a_relu_cap_gate_kernel(tc, qT, kT, t, v, og, out):
     nc = tc.nc
-    others = lambda c: [(h, c) for h in range(1, H)]
-    units = [(0, 0), (0, 1)] + others(0) + [(0, 2)] + others(1) + [(0, 3)] + others(2) + others(3)
+
+    def other_heads(c):
+        return [(h, c) for h in range(1, H)]
+
+    units = [(0, 0), (0, 1)] + other_heads(0) + [(0, 2)] + other_heads(1) + [(0, 3)] + other_heads(2) + other_heads(3)
     last = len(units) - 1
-    groups = [[0, 1], [2, 3, 4, 5], [6, 7, 8, 9], [10, 11, 12], [13, 14], [15]]
+    full_groups = [list(range(u, u + BANK_UNITS)) for u in range(0, last - 3, BANK_UNITS)]
+    groups = full_groups + [[last - 3, last - 2], [last - 1], [last]]
     group_of = {u: (g, i) for g, us in enumerate(groups) for i, u in enumerate(us)}
 
     with ExitStack() as ctx:
@@ -42,11 +53,11 @@ def tile_rows_a_relu_cap_gate_kernel(tc, qT, kT, t, v, og, out):
         og_rows = og.rearrange("h (c q) e -> q h c e", q=QB)
         out_rows = out.rearrange("h (c q) e -> q h c e", q=QB)
 
-        q_raw = [new("q_raw%d" % c, [P, PACK, QB], F32) for c in range(NC)]
-        q_bf = [new("q_bf%d" % c, [P, QB * PACK], BF16) for c in range(NC)]
-        q_codes = [new("q_codes%d" % c, [P, QB], U32) for c in range(NC)]
-        q_scales = [new("q_scales%d" % c, [P, QB], U8) for c in range(NC)]
-        k_raw = [new("k_raw%d" % i, [ROWS, PACK, N // 2], F32) for i in range(2)]
+        q_raw = [new("q_raw%d" % i, [P, PACK, (b - a) * QB], F32) for i, (a, b) in enumerate(Q_PARTS)]
+        q_bf = [new("q_bf%d" % i, [P, (b - a) * QB * PACK], BF16) for i, (a, b) in enumerate(Q_PARTS)]
+        q_codes = [new("q_codes%d" % i, [P, (b - a) * QB], U32) for i, (a, b) in enumerate(Q_PARTS)]
+        q_scales = [new("q_scales%d" % i, [P, (b - a) * QB], U8) for i, (a, b) in enumerate(Q_PARTS)]
+        k_raw = [new("k_raw%d" % half, [ROWS, PACK, N // 2], F32) for half in range(2)]
         k_bf = new("k_bf", [ROWS, N * PACK], BF16)
         k_mx = new("k_mx", [P, N + N // 4], U32)
         k_scales = k_mx[:, N:].bitcast(U8)
@@ -56,49 +67,77 @@ def tile_rows_a_relu_cap_gate_kernel(tc, qT, kT, t, v, og, out):
         v_bf = new("v_bf", [P, E * PACK], BF16)
         v_codes = new("v_codes", [P, E], U32)
         v_scales = new("v_scales", [P, E], U8)
-        og_first = new("og_first", [P, E], F32)
-        og_head0 = new("og_head0", [P, NC - 1, E], F32)
-        og_rest = [new("og_rest%d" % c, [P, H - 1, E], F32) for c in range(NC)]
+        og_raw = new("og_raw", [P, len(units) * E], F32)
         gate = new("gate", [P, len(units) * E], F32)
-        capped = [new("capped%d" % u, [P, QB * PACK], F32) for u in range(len(units))]
-        w_bf = [new("w_bf%d" % u, [P, QB * PACK], BF16) for u in range(len(units))]
-        w_codes = [new("w_codes%d" % u, [P, QB], U32) for u in range(len(units))]
-        w_scales = [new("w_scales%d" % u, [P, QB], U8) for u in range(len(units))]
+        capped = [new("capped%d" % u, [P, WIDE], F32) for u in range(len(units))]
+        w_bf = [new("w_bf%d" % i, [P, 2 * WIDE], BF16) for i in range(len(units) // 2)]
+        w_codes = [new("w_codes%d" % i, [P, 2 * QB], U32) for i in range(len(units) // 2)]
+        w_scales = [new("w_scales%d" % i, [P, 2 * QB], U8) for i in range(len(units) // 2)]
         result = [new("result%d" % g, [P, len(us), E], F32) for g, us in enumerate(groups)]
 
         score_banks = [ps.tile([P, PACK, QB], F32, name="scores%d" % i) for i in range(H + 1)]
-        y_banks = [ps.tile([P, 4, E], F32, name="y%d" % i) for i in range(3)]
+        y_banks = [ps.tile([P, BANK_UNITS, E], F32, name="y%d" % i) for i in range(Y_BANKS)]
 
         def score_bank(u):
             h, c = units[u]
             return score_banks[c % 2] if h == 0 else score_banks[h + 1]
 
-        def load_q(c):
-            nc.sync.dma_start(out=q_raw[c][:], in_=q_rows[:, :, c * QB : (c + 1) * QB])
+        def of_units(tiles, u, n, width):
+            return tiles[u // 2][:, (u % 2) * width : (u % 2 + n) * width]
 
-        def interleave(copy, dst, src):
-            copy(out=dst.rearrange("p (c i j) -> p c j i", i=4, j=PACK), in_=src.rearrange("p j (c i) -> p c j i", i=4))
+        def runs_of(us):
+            runs = []
+            for u in us:
+                h, c = units[u]
+                if runs and runs[-1][2] == c and runs[-1][1] + runs[-1][3] == h:
+                    runs[-1][3] += 1
+                else:
+                    runs.append([u, h, c, 1])
+            return runs
 
-        def quantize(codes, scales, values):
-            nc.vector.quantize_mx(out=codes.bitcast(FP8X4), scales=scales, in_=values)
+        def load_q(i):
+            a, b = Q_PARTS[i]
+            nc.sync.dma_start(out=q_raw[i][:], in_=q_rows[:, :, a * QB : b * QB])
 
-        def quantize_q(c):
-            quantize(q_codes[c][:], q_scales[c][:], q_bf[c][:])
+        def load_og(us):
+            for u, h, c, n in runs_of(us):
+                dst = og_raw[:, u * E : (u + n) * E].rearrange("p (h e) -> p h e", e=E)
+                nc.sync.dma_start(out=dst, in_=og_rows[:, h : h + n, c, :])
+
+        def interleave(dst, src):
+            nc.vector.tensor_copy(
+                out=dst.rearrange("p (c i j) -> p c j i", i=4, j=PACK), in_=src.rearrange("p j (c i) -> p c j i", i=4)
+            )
 
         def deal_keys(half):
-            dst = k_bf[:].rearrange("p (r s j) -> p s r j", r=PACK, j=PACK)[:, 64 * half : 64 * (half + 1)]
+            dst = k_bf[:].rearrange("p (r s j) -> p s r j", r=PACK, j=PACK)[:, half * P // 2 : (half + 1) * P // 2]
             nc.vector.tensor_copy(out=dst, in_=k_raw[half][:].rearrange("p j (s r) -> p s r j", r=PACK))
+
+        def quantize(codes, scales, values_bf):
+            nc.vector.quantize_mx(out=codes.bitcast(FP8X4), scales=scales, in_=values_bf)
+
+        def quantize_k(r):
+            words = slice(r * P, (r + 1) * P)
+            quantize(k_mx[0:ROWS, words], k_scales[0:ROWS, words], k_bf[:, r * P * PACK : (r + 1) * P * PACK])
+
+        def quantize_q(i):
+            quantize(q_codes[i][:], q_scales[i][:], q_bf[i][:])
+
+        def quantize_w(u, n):
+            quantize(of_units(w_codes, u, n, QB), of_units(w_scales, u, n, QB), of_units(w_bf, u, n, WIDE))
 
         def scores(u, r):
             h, c = units[u]
+            i = [n for n, (a, b) in enumerate(Q_PARTS) if a <= c < b][0]
+            queries = slice((c - Q_PARTS[i][0]) * QB, (c - Q_PARTS[i][0] + 1) * QB)
             rows = slice(ROWS * h, ROWS * (h + 1))
-            toks = slice(r * P, (r + 1) * P)
+            words = slice(r * P, (r + 1) * P)
             nc.tensor.matmul_mx(
                 out=score_bank(u)[:, r, :],
-                lhsT=k_mx[rows, toks].bitcast(FP8X4),
-                lhsT_scale=k_scales[rows, toks],
-                rhs=q_codes[c][rows, :].bitcast(FP8X4),
-                rhs_scale=q_scales[c][rows, :],
+                lhsT=k_mx[rows, words].bitcast(FP8X4),
+                lhsT_scale=k_scales[rows, words],
+                rhs=q_codes[i][rows, queries].bitcast(FP8X4),
+                rhs_scale=q_scales[i][rows, queries],
                 start=True,
                 stop=True,
             )
@@ -113,7 +152,7 @@ def tile_rows_a_relu_cap_gate_kernel(tc, qT, kT, t, v, og, out):
 
         def weigh(u):
             nc.vector.scalar_tensor_tensor(
-                out=w_bf[u][:].rearrange("p (n r) -> p n r", r=PACK),
+                out=of_units(w_bf, u, 1, WIDE).rearrange("p (n r) -> p n r", r=PACK),
                 in0=capped[u][:].rearrange("p (n r) -> p n r", r=PACK),
                 scalar=0.0,
                 in1=t_twice[:].unsqueeze(1).to_broadcast([P, QB, PACK]),
@@ -121,75 +160,71 @@ def tile_rows_a_relu_cap_gate_kernel(tc, qT, kT, t, v, og, out):
                 op1=ALU.mult,
             )
 
-        def quantize_w(u):
-            quantize(w_codes[u][:], w_scales[u][:], w_bf[u][:])
+        def values(us):
+            for u in us:
+                g, i = group_of[u]
+                nc.tensor.matmul_mx(
+                    out=y_banks[g % Y_BANKS][:, i, :],
+                    lhsT=of_units(w_codes, u, 1, QB).bitcast(FP8X4),
+                    lhsT_scale=of_units(w_scales, u, 1, QB),
+                    rhs=v_codes[:].bitcast(FP8X4),
+                    rhs_scale=v_scales[:],
+                    start=True,
+                    stop=True,
+                )
 
-        def values(u):
-            g, i = group_of[u]
-            nc.tensor.matmul_mx(
-                out=y_banks[g % 3][:, i, :],
-                lhsT=w_codes[u][:].bitcast(FP8X4),
-                lhsT_scale=w_scales[u][:],
-                rhs=v_codes[:].bitcast(FP8X4),
-                rhs_scale=v_scales[:],
-                start=True,
-                stop=True,
-            )
-
-        def sigmoid_others(c):
-            u = units.index((1, c))
-            nc.scalar.activation(
-                out=gate[:, u * E : (u + H - 1) * E], in_=og_rest[c][:].rearrange("p h e -> p (h e)"), func=ACT.Sigmoid
-            )
+        def sigmoid(us):
+            cols = slice(us[0] * E, (us[-1] + 1) * E)
+            nc.scalar.activation(out=gate[:, cols], in_=og_raw[:, cols], func=ACT.Sigmoid)
 
         def finish(g, queue):
             us = groups[g]
             nc.vector.scalar_tensor_tensor(
                 out=result[g][:].rearrange("p u e -> p (u e)"),
-                in0=y_banks[g % 3][:, 0 : len(us), :].rearrange("p u e -> p (u e)"),
+                in0=y_banks[g % Y_BANKS][:, 0 : len(us), :].rearrange("p u e -> p (u e)"),
                 scalar=1.0 / 16.0,
                 in1=gate[:, us[0] * E : (us[-1] + 1) * E],
                 op0=ALU.mult,
                 op1=ALU.mult,
             )
-            rest = [i for i, u in enumerate(us) if units[u][0] > 0]
-            zero = [i for i, u in enumerate(us) if units[u][0] == 0]
-            if rest:
-                h, c = units[us[rest[0]]]
-                queue.dma_start(out=out_rows[:, h : h + len(rest), c, :], in_=result[g][:, rest[0] : rest[-1] + 1, :])
-            if zero:
-                c = units[us[zero[0]]][1]
-                queue.dma_start(out=out_rows[:, 0, c : c + len(zero), :], in_=result[g][:, zero[0] : zero[-1] + 1, :])
+            for u, h, c, n in runs_of(us):
+                queue.dma_start(out=out_rows[:, h : h + n, c, :], in_=result[g][:, u - us[0] : u - us[0] + n, :])
 
         nc.gpsimd.memset(k_mx[0:ROWS, N:], 0)
-        for half in range(2):
-            nc.sync.dma_start(out=k_raw[half][:], in_=k_rows[:, :, half * (N // 2) : (half + 1) * (N // 2)])
-        nc.scalar.dma_start(out=og_first[:], in_=og_rows[:, 0, 0, :])
-        nc.scalar.dma_start(out=t_raw[:], in_=t.rearrange("(p j) o -> p (j o)", j=PACK))
-        for c in range(3):
-            load_q(c)
 
-        nc.scalar.activation(out=gate[:, 0:E], in_=og_first[:], func=ACT.Sigmoid)
+        for half in range(2):
+            nc.sync.dma_start(out=k_raw[half][:], in_=k_rows[:, :, half * N // 2 : (half + 1) * N // 2])
+        load_q(0)
+        load_q(1)
+        load_og([0])
+        nc.sync.dma_start(out=t_raw[:], in_=t.rearrange("(p j) o -> p (j o)", j=PACK))
+        load_q(2)
+
+        sigmoid([0])
         nc.scalar.mul(out=t_twice[:], in_=t_raw[:], mul=2.0)
-        interleave(nc.scalar.copy, q_bf[0][:], q_raw[0][:])
+
         deal_keys(0)
         deal_keys(1)
-        quantize(k_mx[0:ROWS, 0:N], k_scales[0:ROWS, :], k_bf[:])
+        interleave(q_bf[0][:], q_raw[0][:])
+        quantize_k(0)
         quantize_q(0)
+        for r in range(1, PACK):
+            quantize_k(r)
         for h in range(1, H):
             nc.sync.dma_start(out=k_mx[ROWS * h : ROWS * (h + 1), :].bitcast(I32), in_=k_mx[0:ROWS, :].bitcast(I32))
         nc.sync.dma_start(out=v_raw[:], in_=v.rearrange("o (p j) e -> (o p) j e", j=PACK))
-        load_q(3)
-        nc.sync.dma_start(out=og_head0[:], in_=og_rows[:, 0, 1:, :])
-        for c in range(NC):
-            nc.sync.dma_start(out=og_rest[c][:], in_=og_rows[:, 1:, c, :])
-
-        interleave(nc.vector.tensor_copy, q_bf[1][:], q_raw[1][:])
+        load_og(list(range(1, len(units))))
+        interleave(q_bf[1][:], q_raw[1][:])
         quantize_q(1)
-        interleave(nc.vector.tensor_copy, q_bf[2][:], q_raw[2][:])
+
         for u in range(3):
             for r in range(PACK):
                 scores(u, r)
+
+        values_at = {min(us[-1] + VALUES_LAG, last - 2): us for us in full_groups}
+        finish_at = {min(us[-1] + FINISH_LAG, last - 1): g for g, us in enumerate(full_groups)}
+        sigmoid_at = {s - SIGMOID_LEAD: [u for u in groups[g] if u > 0] for s, g in finish_at.items()}
+        sigmoid_at[last] = list(range(last - 3, last + 1))
 
         for step in range(len(units)):
             cap(step)
@@ -198,38 +233,30 @@ def tile_rows_a_relu_cap_gate_kernel(tc, qT, kT, t, v, og, out):
                     scores(step + 3, r)
                 if 3 <= step + 2 <= last:
                     scores(step + 2, r + 2)
-            if step == 3:
-                interleave(nc.scalar.copy, v_bf[:], v_raw[:])
-            if step == 5:
-                nc.scalar.activation(
-                    out=gate[:].rearrange("p (a u e) -> p a u e", u=4, e=E)[:, 0:3, 1, :], in_=og_head0[:], func=ACT.Sigmoid
-                )
-            if step in (7, 10, 12, 14):
-                sigmoid_others((7, 10, 12, 14).index(step))
+            if step in sigmoid_at:
+                sigmoid(sigmoid_at[step])
+
             weigh(step)
             if step == 0:
+                interleave(q_bf[2][:], q_raw[2][:])
+            if step == 1:
                 quantize_q(2)
-            if step > 0:
-                quantize_w(step - 1)
-            if step == 3:
-                interleave(nc.vector.tensor_copy, q_bf[3][:], q_raw[3][:])
-            if step == 4:
-                quantize_q(3)
-            if step == 5:
+                interleave(v_bf[:], v_raw[:])
+            if step >= 2 and step % 2 == 0:
+                quantize_w(step - 2, 2)
+            if step == 2:
                 quantize(v_codes[:], v_scales[:], v_bf[:])
-            if step in (6, 8, 12):
-                g = (6, 8, 12).index(step)
-                for u in groups[g]:
-                    values(u)
-                finish(g, nc.sync)
-            if step == 13:
-                for u in groups[3]:
-                    values(u)
-            if step == 14:
-                finish(3, nc.sync)
-            if step >= 14:
-                values(step - 1)
-        quantize_w(last)
-        values(last)
-        finish(4, nc.sync)
-        finish(5, nc.scalar)
+
+            if step in values_at:
+                values(values_at[step])
+            if step in finish_at:
+                finish(finish_at[step], nc.sync)
+            if step == last - 1:
+                values(groups[-3])
+
+        for u in (last - 1, last):
+            quantize_w(u, 1)
+            values([u])
+        finish(len(groups) - 3, nc.sync)
+        finish(len(groups) - 2, nc.sync)
+        finish(len(groups) - 1, nc.scalar)

from contextlib import ExitStack

import concourse.mybir as mybir

H, D, NQ, N, E = 4, 128, 512, 512, 128
FLOPS = 2 * H * N * NQ * D + 2 * H * N * NQ * E

F32 = mybir.dt.float32
BF16 = mybir.dt.bfloat16
U32 = mybir.dt.uint32
I32 = mybir.dt.int32
U8 = mybir.dt.uint8
FP8X4 = mybir.dt.float8_e4m3fn_x4
ACT = mybir.ActivationFunctionType
ALU = mybir.AluOpType

P = 128
PACK = 4
ROWS = D // PACK
QB = 128
WIDE = QB * PACK
BANK_UNITS = 4
Y_BANKS = 3

Q_PARTS = [(0, 1), (1, 2), (2, 4)]
VALUES_LAG = 3
FINISH_LAG = 4
SIGMOID_LEAD = 2


def tile_rows_a_relu_cap_gate_kernel(tc, qT, kT, t, v, og, out):
    nc = tc.nc

    def other_heads(c):
        return [(h, c) for h in range(1, H)]

    units = [(0, 0), (0, 1)] + other_heads(0) + [(0, 2)] + other_heads(1) + [(0, 3)] + other_heads(2) + other_heads(3)
    last = len(units) - 1
    full_groups = [list(range(u, u + BANK_UNITS)) for u in range(0, last - 3, BANK_UNITS)]
    groups = full_groups + [[last - 3, last - 2], [last - 1], [last]]
    group_of = {u: (g, i) for g, us in enumerate(groups) for i, u in enumerate(us)}

    with ExitStack() as ctx:
        sb = ctx.enter_context(tc.tile_pool(name="sb", bufs=1))
        ps = ctx.enter_context(tc.psum_pool(name="ps", bufs=1))
        ctx.enter_context(tc.manual_schedule())

        def new(name, shape, dtype):
            return sb.tile(shape, dtype, name=name, align_bytes=64)

        q_rows = qT.rearrange("h (p j) n -> (h p) j n", j=PACK)
        k_rows = kT.rearrange("o (p j) n -> (o p) j n", j=PACK)
        og_rows = og.rearrange("h (c q) e -> q h c e", q=QB)
        out_rows = out.rearrange("h (c q) e -> q h c e", q=QB)

        q_raw = [new("q_raw%d" % i, [P, PACK, (b - a) * QB], F32) for i, (a, b) in enumerate(Q_PARTS)]
        q_bf = [new("q_bf%d" % i, [P, (b - a) * QB * PACK], BF16) for i, (a, b) in enumerate(Q_PARTS)]
        q_codes = [new("q_codes%d" % i, [P, (b - a) * QB], U32) for i, (a, b) in enumerate(Q_PARTS)]
        q_scales = [new("q_scales%d" % i, [P, (b - a) * QB], U8) for i, (a, b) in enumerate(Q_PARTS)]
        k_raw = [new("k_raw%d" % half, [ROWS, PACK, N // 2], F32) for half in range(2)]
        k_bf = new("k_bf", [ROWS, N * PACK], BF16)
        k_mx = new("k_mx", [P, N + N // 4], U32)
        k_scales = k_mx[:, N:].bitcast(U8)
        t_raw = new("t_raw", [P, PACK], F32)
        t_twice = new("t_twice", [P, PACK], F32)
        v_raw = new("v_raw", [P, PACK, E], F32)
        v_bf = new("v_bf", [P, E * PACK], BF16)
        v_codes = new("v_codes", [P, E], U32)
        v_scales = new("v_scales", [P, E], U8)
        og_raw = new("og_raw", [P, len(units) * E], F32)
        gate = new("gate", [P, len(units) * E], F32)
        capped = [new("capped%d" % u, [P, WIDE], F32) for u in range(len(units))]
        w_bf = [new("w_bf%d" % i, [P, 2 * WIDE], BF16) for i in range(len(units) // 2)]
        w_codes = [new("w_codes%d" % i, [P, 2 * QB], U32) for i in range(len(units) // 2)]
        w_scales = [new("w_scales%d" % i, [P, 2 * QB], U8) for i in range(len(units) // 2)]
        result = [new("result%d" % g, [P, len(us), E], F32) for g, us in enumerate(groups)]

        score_banks = [ps.tile([P, PACK, QB], F32, name="scores%d" % i) for i in range(H + 1)]
        y_banks = [ps.tile([P, BANK_UNITS, E], F32, name="y%d" % i) for i in range(Y_BANKS)]

        def score_bank(u):
            h, c = units[u]
            return score_banks[c % 2] if h == 0 else score_banks[h + 1]

        def of_units(tiles, u, n, width):
            return tiles[u // 2][:, (u % 2) * width : (u % 2 + n) * width]

        def runs_of(us):
            runs = []
            for u in us:
                h, c = units[u]
                if runs and runs[-1][2] == c and runs[-1][1] + runs[-1][3] == h:
                    runs[-1][3] += 1
                else:
                    runs.append([u, h, c, 1])
            return runs

        def load_q(i):
            a, b = Q_PARTS[i]
            nc.sync.dma_start(out=q_raw[i][:], in_=q_rows[:, :, a * QB : b * QB])

        def load_og(us):
            for u, h, c, n in runs_of(us):
                dst = og_raw[:, u * E : (u + n) * E].rearrange("p (h e) -> p h e", e=E)
                nc.sync.dma_start(out=dst, in_=og_rows[:, h : h + n, c, :])

        def interleave(dst, src):
            nc.vector.tensor_copy(
                out=dst.rearrange("p (c i j) -> p c j i", i=4, j=PACK), in_=src.rearrange("p j (c i) -> p c j i", i=4)
            )

        def deal_keys(half):
            dst = k_bf[:].rearrange("p (r s j) -> p s r j", r=PACK, j=PACK)[:, half * P // 2 : (half + 1) * P // 2]
            nc.vector.tensor_copy(out=dst, in_=k_raw[half][:].rearrange("p j (s r) -> p s r j", r=PACK))

        def quantize(codes, scales, values_bf):
            nc.vector.quantize_mx(out=codes.bitcast(FP8X4), scales=scales, in_=values_bf)

        def quantize_k(r):
            words = slice(r * P, (r + 1) * P)
            quantize(k_mx[0:ROWS, words], k_scales[0:ROWS, words], k_bf[:, r * P * PACK : (r + 1) * P * PACK])

        def quantize_q(i):
            quantize(q_codes[i][:], q_scales[i][:], q_bf[i][:])

        def quantize_w(u, n):
            quantize(of_units(w_codes, u, n, QB), of_units(w_scales, u, n, QB), of_units(w_bf, u, n, WIDE))

        def scores(u, r):
            h, c = units[u]
            i = [n for n, (a, b) in enumerate(Q_PARTS) if a <= c < b][0]
            queries = slice((c - Q_PARTS[i][0]) * QB, (c - Q_PARTS[i][0] + 1) * QB)
            rows = slice(ROWS * h, ROWS * (h + 1))
            words = slice(r * P, (r + 1) * P)
            nc.tensor.matmul_mx(
                out=score_bank(u)[:, r, :],
                lhsT=k_mx[rows, words].bitcast(FP8X4),
                lhsT_scale=k_scales[rows, words],
                rhs=q_codes[i][rows, queries].bitcast(FP8X4),
                rhs_scale=q_scales[i][rows, queries],
                start=True,
                stop=True,
            )

        def cap(u):
            nc.scalar.activation(
                out=capped[u][:].rearrange("p (n r) -> p n r", r=PACK),
                in_=score_bank(u)[:].rearrange("p r n -> p n r"),
                func=ACT.Tanh,
                scale=0.5,
            )

        def weigh(u):
            nc.vector.scalar_tensor_tensor(
                out=of_units(w_bf, u, 1, WIDE).rearrange("p (n r) -> p n r", r=PACK),
                in0=capped[u][:].rearrange("p (n r) -> p n r", r=PACK),
                scalar=0.0,
                in1=t_twice[:].unsqueeze(1).to_broadcast([P, QB, PACK]),
                op0=ALU.max,
                op1=ALU.mult,
            )

        def values(us):
            for u in us:
                g, i = group_of[u]
                nc.tensor.matmul_mx(
                    out=y_banks[g % Y_BANKS][:, i, :],
                    lhsT=of_units(w_codes, u, 1, QB).bitcast(FP8X4),
                    lhsT_scale=of_units(w_scales, u, 1, QB),
                    rhs=v_codes[:].bitcast(FP8X4),
                    rhs_scale=v_scales[:],
                    start=True,
                    stop=True,
                )

        def sigmoid(us):
            cols = slice(us[0] * E, (us[-1] + 1) * E)
            nc.scalar.activation(out=gate[:, cols], in_=og_raw[:, cols], func=ACT.Sigmoid)

        def finish(g, queue):
            us = groups[g]
            nc.vector.scalar_tensor_tensor(
                out=result[g][:].rearrange("p u e -> p (u e)"),
                in0=y_banks[g % Y_BANKS][:, 0 : len(us), :].rearrange("p u e -> p (u e)"),
                scalar=1.0 / 16.0,
                in1=gate[:, us[0] * E : (us[-1] + 1) * E],
                op0=ALU.mult,
                op1=ALU.mult,
            )
            for u, h, c, n in runs_of(us):
                queue.dma_start(out=out_rows[:, h : h + n, c, :], in_=result[g][:, u - us[0] : u - us[0] + n, :])

        nc.gpsimd.memset(k_mx[0:ROWS, N:], 0)

        for half in range(2):
            nc.sync.dma_start(out=k_raw[half][:], in_=k_rows[:, :, half * N // 2 : (half + 1) * N // 2])
        load_q(0)
        load_q(1)
        load_og([0])
        nc.sync.dma_start(out=t_raw[:], in_=t.rearrange("(p j) o -> p (j o)", j=PACK))
        load_q(2)

        sigmoid([0])
        nc.scalar.mul(out=t_twice[:], in_=t_raw[:], mul=2.0)

        deal_keys(0)
        deal_keys(1)
        interleave(q_bf[0][:], q_raw[0][:])
        quantize_k(0)
        quantize_q(0)
        for r in range(1, PACK):
            quantize_k(r)
        for h in range(1, H):
            nc.sync.dma_start(out=k_mx[ROWS * h : ROWS * (h + 1), :].bitcast(I32), in_=k_mx[0:ROWS, :].bitcast(I32))
        nc.sync.dma_start(out=v_raw[:], in_=v.rearrange("o (p j) e -> (o p) j e", j=PACK))
        load_og(list(range(1, len(units))))
        interleave(q_bf[1][:], q_raw[1][:])
        quantize_q(1)

        for u in range(3):
            for r in range(PACK):
                scores(u, r)

        values_at = {min(us[-1] + VALUES_LAG, last - 2): us for us in full_groups}
        finish_at = {min(us[-1] + FINISH_LAG, last - 1): g for g, us in enumerate(full_groups)}
        sigmoid_at = {s - SIGMOID_LEAD: [u for u in groups[g] if u > 0] for s, g in finish_at.items()}
        sigmoid_at[last] = list(range(last - 3, last + 1))

        for step in range(len(units)):
            cap(step)
            for r in range(2):
                if step + 3 <= last:
                    scores(step + 3, r)
                if 3 <= step + 2 <= last:
                    scores(step + 2, r + 2)
            if step in sigmoid_at:
                sigmoid(sigmoid_at[step])

            weigh(step)
            if step == 0:
                interleave(q_bf[2][:], q_raw[2][:])
            if step == 1:
                quantize_q(2)
                interleave(v_bf[:], v_raw[:])
            if step >= 2 and step % 2 == 0:
                quantize_w(step - 2, 2)
            if step == 2:
                quantize(v_codes[:], v_scales[:], v_bf[:])

            if step in values_at:
                values(values_at[step])
            if step in finish_at:
                finish(finish_at[step], nc.sync)
            if step == last - 1:
                values(groups[-3])

        for u in (last - 1, last):
            quantize_w(u, 1)
            values([u])
        finish(len(groups) - 3, nc.sync)
        finish(len(groups) - 2, nc.sync)
        finish(len(groups) - 1, nc.scalar)
